import numpy as np
import ml_dtypes


def mxq(x, axis, fmt="e4m3"):
    dtype, down = {"e4m3": (ml_dtypes.float8_e4m3fn, 7), "e5m2": (ml_dtypes.float8_e5m2, 14)}[fmt]
    v = np.moveaxis(np.asarray(x, np.float32).astype(ml_dtypes.bfloat16).astype(np.float64), axis, -1)
    blocks = v.reshape(v.shape[:-1] + (-1, 32))
    amax = np.abs(blocks).max(-1, keepdims=True)
    byte = np.maximum(np.where(amax > 0, np.frexp(amax)[1] - 1 + 127, 0) - down, 1)
    scale = np.exp2(byte - 127.0)
    codes = (blocks / scale).astype(np.float32).astype(dtype).astype(np.float64)
    return np.moveaxis((codes * scale).reshape(v.shape), -1, axis)


WIDE = False


def mx_kscale(k):
    if not WIDE:
        return np.ones(k)
    levels = np.array([30, -30])
    if k % 512:
        return np.exp2(np.random.permutation(np.resize(levels, k // 32))).repeat(32)
    a = np.empty((k // 512, 16))
    for p in range(k // 512):
        a[p, :8] = np.random.permutation(np.resize(levels, 8))
        for g in range(8):
            far = levels[np.abs(levels - a[p, g]) >= 10]
            a[p, g + 8] = far[np.random.randint(len(far))]
    return np.exp2(a.ravel()).repeat(32)


def f64(x):
    return np.asarray(x).astype(np.float64)


def striped(idx):
    return np.tile(np.asarray(idx).reshape(-1, 16).T, (8, 1)).astype(np.uint16)


def unstriped(offs):
    return offs[:16].T.reshape(-1).astype(np.int64)


E2M1 = np.array([0.0, 0.5, 1.0, 1.5, 2.0, 3.0, 4.0, 6.0, -0.0, -0.5, -1.0, -1.5, -2.0, -3.0, -4.0, -6.0])


def pack_weight(w, fmt):
    k, n = w.shape
    w = f64(np.asarray(w, np.float32).astype(ml_dtypes.bfloat16)).reshape(k // 32, 32, n)
    amax = np.abs(w).max(1)
    if fmt in ("e4m3", "e5m2"):
        byte = np.frexp(amax)[1] - 1 + 127 - (7 if fmt == "e4m3" else 14)
    else:
        mant, ex = np.frexp(amax / 6.0)
        byte = np.where(mant > 0.5, ex, ex - 1) + 127
    byte = np.clip(np.where(amax > 0, byte, 1), 1, 254)
    scaled = (w * np.exp2(127.0 - byte)[:, None, :]).reshape(k, n).astype(np.float32)
    by_word = np.ascontiguousarray(scaled.reshape(k // 512, 128, 4, n).transpose(0, 1, 3, 2))
    if fmt in ("e4m3", "e5m2"):
        words = by_word.astype(ml_dtypes.float8_e4m3fn if fmt == "e4m3" else ml_dtypes.float8_e5m2).view(np.uint8)
    else:
        c = by_word.astype(ml_dtypes.float4_e2m1fn).view(np.uint8) & 0xF
        words = (c[..., 0::2] | (c[..., 1::2] << 4)).reshape(k // 512, 128, 2 * n)
    return np.ascontiguousarray(words), np.ascontiguousarray(byte.astype(np.uint8).reshape(k // 512, 16, n))


def unpack_weight(words, scales, fmt):
    g, _, n = scales.shape
    words = np.ascontiguousarray(words).reshape(g, 128, n, -1)
    if fmt in ("e4m3", "e5m2"):
        vals = words.view(ml_dtypes.float8_e4m3fn if fmt == "e4m3" else ml_dtypes.float8_e5m2).astype(np.float64)
    else:
        nib = np.empty((g, 128, n, 4), np.uint8)
        nib[..., 0::2] = words & 0xF
        nib[..., 1::2] = words >> 4
        vals = E2M1[nib]
    vals = vals * np.repeat(np.exp2(scales.astype(np.float64) - 127.0), 8, axis=1)[..., None]
    return vals.transpose(0, 1, 3, 2).reshape(g * 512, n)


def sigmoid(v):
    return 1.0 / (1.0 + np.exp(-v))


def sgn(shape):
    return np.random.uniform(0.5, 2.0, shape) * np.where(np.random.standard_normal(shape) < 0, -1.0, 1.0)


K, T, J, R, F, Z, N, O = 512, 1024, 256, 512, 512, 1024, 256, 128


def setup_inputs():
    n = np.random.standard_normal
    idx = np.random.permutation(T)[:J]
    idx2 = np.random.permutation(Z)[:J]
    idx3 = np.random.permutation(J)[:O]
    idx4 = np.random.permutation(J)[:O]
    fk = mx_kscale(K)
    ff = mx_kscale(F)
    fr = mx_kscale(R)
    xtp = pack_weight(n((K, T)) / fk[:, None], "e5m2")
    xop = pack_weight(n((F, Z)) / ff[:, None], "e4m3")
    wp = pack_weight(n((K, R)) * 1 / np.sqrt(K) * fk[:, None] * fr, "e2m1")
    w2p = pack_weight(n((K, R)) * 1 / np.sqrt(K) * fk[:, None] * fr, "e4m3")
    w0p = pack_weight(n((F, R)) * 1 / np.sqrt(F) * ff[:, None] * fr, "e4m3")
    wbp = pack_weight(n((R, N)) * 1 / np.sqrt(R) / fr[:, None], "e2m1")
    wcp = pack_weight(n((R, N)) * 1 / np.sqrt(R) / fr[:, None], "e4m3")
    return {
        "xt_words": xtp[0],
        "xt_scales": xtp[1],
        "xo_words": xop[0],
        "xo_scales": xop[1],
        "w_words": wp[0],
        "w_scales": wp[1],
        "w2_words": w2p[0],
        "w2_scales": w2p[1],
        "w0_words": w0p[0],
        "w0_scales": w0p[1],
        "wb_words": wbp[0],
        "wb_scales": wbp[1],
        "wc_words": wcp[0],
        "wc_scales": wcp[1],
        "so": (np.random.uniform(0.5, 1.6, (N, 1))).astype(np.float32),
        "sp": (sgn((N, 1))).astype(np.float32),
        "bo": (np.random.uniform(-2.0, 2.0, (N, 1))).astype(np.float32),
        "offs": striped(idx),
        "offs2": striped(idx2),
        "offs3": striped(idx3),
        "offs4": striped(idx4),
    }


def reference(xt_words, xt_scales, xo_words, xo_scales, w_words, w_scales, w2_words, w2_scales, w0_words, w0_scales, wb_words, wb_scales, wc_words, wc_scales, so, sp, bo, offs, offs2, offs3, offs4):
    idx = unstriped(offs)
    idx2 = unstriped(offs2)
    idx3 = unstriped(offs3)
    idx4 = unstriped(offs4)
    xtu = unpack_weight(xt_words, xt_scales, "e5m2")
    xou = unpack_weight(xo_words, xo_scales, "e4m3")
    wu = unpack_weight(w_words, w_scales, "e2m1")
    w2u = unpack_weight(w2_words, w2_scales, "e4m3")
    w0u = unpack_weight(w0_words, w0_scales, "e4m3")
    wbu = unpack_weight(wb_words, wb_scales, "e2m1")
    wcu = unpack_weight(wc_words, wc_scales, "e4m3")
    xtidxg = xtu[:, idx]
    a = wu.T @ xtidxg
    xoidx2g = xou[:, idx2]
    b = w2u.T @ xtidxg + w0u.T @ xoidx2g
    hid = np.maximum(a, b)
    hidq = mxq(hid, 0, "e4m3")
    p = wbu.T @ hidq
    q = wcu.T @ hidq
    m0 = np.maximum(p, q)
    y = m0[:, idx3] * f64(so) * sigmoid(m0[:, idx4] * f64(sp) + f64(bo))
    return y

@@ -1,0 +1,191 @@
+from contextlib import ExitStack
+
+import concourse.mybir as mybir
+
+F32 = mybir.dt.float32
+BF16 = mybir.dt.bfloat16
+I32 = mybir.dt.int32
+U32 = mybir.dt.uint32
+U16 = mybir.dt.uint16
+U8 = mybir.dt.uint8
+E4M3 = mybir.dt.float8_e4m3fn_x4
+E5M2 = mybir.dt.float8_e5m2_x4
+E2M1 = mybir.dt.float4_e2m1fn_x4
+ACT = mybir.ActivationFunctionType
+ALU = mybir.AluOpType
+
+P = 128
+T, J, R, N, O = 1024, 256, 512, 256, 128
+HALF = 128
+FLOPS = 2 * 512 * J * (3 * R + 2 * N)
+
+
+def tile_list_outcomegatedmeet_leaned_kernel(
+    tc, xt_words, xt_scales, xo_words, xo_scales, w_words, w_scales, w2_words, w2_scales,
+    w0_words, w0_scales, wb_words, wb_scales, wc_words, wc_scales, so, sp, bo,
+    offs, offs2, offs3, offs4, out,
+):
+    nc = tc.nc
+    with ExitStack() as ctx:
+        keep = ctx.enter_context(tc.tile_pool(name="keep", bufs=1))
+        psum = ctx.enter_context(tc.psum_pool(name="psum", bufs=1))
+
+        def sb(name, shape, dtype):
+            return keep.tile(shape, dtype, name=name, align_bytes=64)
+
+        def words32(dram):
+            return dram[0].rearrange("p c r -> p (c r)").bitcast(I32)
+
+        def staged_rows(dram):
+            return dram[0].bitcast(I32).rearrange("(q r) c -> r q c", r=4)
+
+        def load_rows(queue, plane, first, dram):
+            rows = dram[0].bitcast(I32)
+            for q in range(4):
+                queue.dma_start(out=plane[32 * q + first : 32 * q + first + 4, :].bitcast(I32), in_=rows[4 * q : 4 * q + 4, :])
+
+        list1 = sb("list1", [P, J // 16], U16)
+        list2 = sb("list2", [P, J // 16], U16)
+        list3 = sb("list3", [P, O // 16], U16)
+        list4 = sb("list4", [P, O // 16], U16)
+        xt_w = sb("xt_w", [P, T], U32)
+        xo_w = sb("xo_w", [P, T], U32)
+        xt_s = sb("xt_s", [P, T], U8)
+        xo_s = sb("xo_s", [P, T], U8)
+        xt_stage = sb("xt_stage", [4, 4, T // 4], I32)
+        w_stage = sb("w_stage", [4, 4, R // 4], I32)
+        pair_stage = sb("pair_stage", [32, 4, R // 4], I32)
+        w_spread = sb("w_spread", [P, R // 4], I32)
+        pair_spread = sb("pair_spread", [P, R // 4], I32)
+        w_raw = sb("w_raw", [P, R], U16)
+        w2_raw = sb("w2_raw", [P, R], U32)
+        w0_raw = sb("w0_raw", [P, R], U32)
+        w_w = sb("w_w", [P, R], U16)
+        w2_w = sb("w2_w", [P, R], U32)
+        w0_w = sb("w0_w", [P, R], U32)
+        w_s = sb("w_s", [P, R], U8)
+        pair_s = sb("pair_s", [P, R], U8)
+        wb_w = sb("wb_w", [P, N], U16)
+        wc_w = sb("wc_w", [P, N], U32)
+        wb_s = sb("wb_s", [P, N], U8)
+        wc_s = sb("wc_s", [P, N], U8)
+        so_t = sb("so_t", [P, 2], F32)
+        sp_t = sb("sp_t", [P, 2], F32)
+        bo_t = sb("bo_t", [P, 2], F32)
+
+        nc.vector.memset(pair_stage[:], 0)
+        nc.vector.memset(xo_s[:].bitcast(I32), 0)
+        nc.gpsimd.memset(wb_s[:].bitcast(I32), 0)
+        nc.gpsimd.memset(wc_s[:].bitcast(I32), 0)
+        nc.vector.memset(xt_s[:].bitcast(I32), 0)
+        nc.vector.memset(w_spread[:], 0)
+
+        nc.sync.dma_start(list1[:], offs)
+        nc.scalar.dma_start(out=xt_stage[:], in_=staged_rows(xt_scales))
+        nc.scalar.dma_start(out=w_stage[:], in_=staged_rows(w_scales))
+        nc.sync.dma_start(out=xt_w[:].bitcast(I32), in_=words32(xt_words))
+        nc.sync.dma_start(out=pair_stage[0:4], in_=staged_rows(w2_scales))
+        nc.sync.dma_start(out=pair_stage[4:8], in_=staged_rows(w0_scales))
+        nc.sync.dma_start(out=w_raw[:].bitcast(I32), in_=w_words[0].bitcast(I32))
+        nc.sync.dma_start(out=w2_raw[:].bitcast(I32), in_=words32(w2_words))
+        load_rows(nc.sync, xo_s, 4, xo_scales)
+        nc.sync.dma_start(out=xo_w[:].bitcast(I32), in_=words32(xo_words))
+        nc.sync.dma_start(list2[:], offs2)
+        nc.sync.dma_start(out=w0_raw[:].bitcast(I32), in_=words32(w0_words))
+        nc.sync.dma_start(out=wb_w[:].bitcast(I32), in_=wb_words[0].bitcast(I32))
+        nc.sync.dma_start(out=wc_w[:].bitcast(I32), in_=words32(wc_words))
+        load_rows(nc.gpsimd, wb_s, 0, wb_scales)
+        load_rows(nc.sync, wc_s, 0, wc_scales)
+        nc.sync.dma_start(list4[:], offs4)
+        nc.sync.dma_start(list3[:], offs3)
+        with nc.allow_non_contiguous_dma(reason="one value a partition"):
+            for queue, tile, vec in ((nc.gpsimd, sp_t, sp), (nc.gpsimd, bo_t, bo), (nc.sync, so_t, so)):
+                queue.dma_start(out=tile[:], in_=vec.rearrange("(c p) o -> p (c o)", p=P))
+
+        def spread(dst, stage, rows):
+            for q in range(4):
+                nc.vector.tensor_copy(out=dst[32 * q : 32 * q + rows, :], in_=stage[0:rows, q, :])
+
+        def deal_by_read(copy, dst, src):
+            copy(out=dst.rearrange("p (t m) -> p t m", t=4), in_=src.rearrange("p (m t) -> p t m", t=4))
+
+        def deal_by_write(copy, dst, src):
+            copy(out=dst.rearrange("p (t m) -> p m t", t=4), in_=src.rearrange("p (m t) -> p m t", t=4))
+
+        def gather(name, words, scales, offsets, h):
+            gw = sb(name + "_gw%d" % h, [P, HALF], U32)
+            gs = sb(name + "_gs%d" % h, [P, HALF], U8)
+            part = offsets[:, 8 * h : 8 * h + 8]
+            nc.vector.tensor_copy(out=gw[:], in_=words[:].indirect(part))
+            nc.vector.tensor_copy(out=gs[:], in_=scales[:].indirect(part))
+            return gw, gs
+
+        spread(xt_s[:].bitcast(I32), xt_stage, 4)
+        spread(w_spread, w_stage, 4)
+        deal_by_read(nc.vector.tensor_copy, w_s[:], w_spread[:].bitcast(U8))
+        deal_by_read(nc.scalar.copy, w_w[:], w_raw[:])
+        deal_by_write(nc.scalar.copy, w2_w[:], w2_raw[:])
+
+        a_ps = [psum.tile([P, 4, HALF], F32, name="a_ps%d" % h) for h in range(2)]
+        b_ps = [psum.tile([P, 4, HALF], F32, name="b_ps%d" % h) for h in range(2)]
+        a_sb = [sb("a_sb%d" % h, [P, HALF, 4], F32) for h in range(2)]
+
+        xg = [gather("xt", xt_w, xt_s, list1, 0)]
+        spread(pair_spread, pair_stage, 32)
+        deal_by_read(nc.vector.tensor_copy, pair_s[:], pair_spread[:].bitcast(U8))
+        xg.append(gather("xt", xt_w, xt_s, list1, 1))
+        for h in range(2):
+            gw, gs = xg[h]
+            for t in range(4):
+                cols = slice(P * t, P * t + P)
+                nc.tensor.matmul_mx(out=a_ps[h][:, t, :], lhsT=w_w[:, cols].bitcast(E2M1), lhsT_scale=w_s[:, cols],
+                                    rhs=gw[:].bitcast(E5M2), rhs_scale=gs[:], start=True, stop=True)
+            for t in range(4):
+                cols = slice(P * t, P * t + P)
+                nc.tensor.matmul_mx(out=b_ps[h][:, t, :], lhsT=w2_w[:, cols].bitcast(E4M3), lhsT_scale=pair_s[:, cols],
+                                    rhs=gw[:].bitcast(E5M2), rhs_scale=gs[:], start=(t == 0), stop=False)
+        deal_by_write(nc.scalar.copy, w0_w[:], w0_raw[:])
+        for h in range(2):
+            nc.scalar.copy(out=a_sb[h][:], in_=a_ps[h][:].rearrange("p t j -> p j t"))
+        og = [gather("xo", xo_w, xo_s, list2, h) for h in range(2)]
+        for h in range(2):
+            gw, gs = og[h]
+            for t in range(4):
+                cols = slice(P * t, P * t + P)
+                nc.tensor.matmul_mx(out=b_ps[h][:, t, :], lhsT=w0_w[:, cols].bitcast(E4M3), lhsT_scale=pair_s[4:P, cols],
+                                    rhs=gw[:].bitcast(E4M3), rhs_scale=gs[4:P, :], start=False, stop=(t == 3))
+
+        hid = [sb("hid%d" % h, [P, HALF, 4], BF16) for h in range(2)]
+        hq_w = [sb("hq_w%d" % h, [P, HALF], U32) for h in range(2)]
+        hq_s = [sb("hq_s%d" % h, [P, HALF], U8) for h in range(2)]
+        for h in range(2):
+            nc.vector.tensor_tensor(out=hid[h][:], in0=b_ps[h][:].rearrange("p t j -> p j t"), in1=a_sb[h][:], op=ALU.max)
+        for h in range(2):
+            nc.vector.quantize_mx(out=hq_w[h][:].bitcast(E4M3), scales=hq_s[h][:], in_=hid[h][:].rearrange("p j t -> p (j t)"))
+
+        low_ps = [psum.tile([P, 2, HALF], F32, name="low_ps%d" % h) for h in range(2)]
+        high_ps = psum.tile([P, 2, 2, HALF], F32, name="high_ps")
+        m0 = [sb("m0_%d" % c, [P, J], F32) for c in range(2)]
+        for h in range(2):
+            for c in range(2):
+                cols = slice(P * c, P * c + P)
+                pq = low_ps[h][:] if c == 0 else high_ps[:, h]
+                nc.tensor.matmul_mx(out=pq[:, 0, :], lhsT=wb_w[:, cols].bitcast(E2M1), lhsT_scale=wb_s[:, cols],
+                                    rhs=hq_w[h][:].bitcast(E4M3), rhs_scale=hq_s[h][:], start=True, stop=True)
+                nc.tensor.matmul_mx(out=pq[:, 1, :], lhsT=wc_w[:, cols].bitcast(E4M3), lhsT_scale=wc_s[:, cols],
+                                    rhs=hq_w[h][:].bitcast(E4M3), rhs_scale=hq_s[h][:], start=True, stop=True)
+        for h in range(2):
+            nc.vector.tensor_reduce(out=m0[0][:, HALF * h : HALF * h + HALF], in_=low_ps[h][:].rearrange("p s j -> p j s"),
+                                    axis=mybir.AxisListType.X, op=ALU.max)
+        nc.vector.tensor_reduce(out=m0[1][:].rearrange("p (h j) -> p h j", h=2), in_=high_ps[:].rearrange("p h s j -> p h j s"),
+                                axis=mybir.AxisListType.X, op=ALU.max)
+
+        for c in range(2):
+            gate = sb("gate%d" % c, [P, O], F32)
+            kept = sb("kept%d" % c, [P, O], F32)
+            y = sb("y%d" % c, [P, O], F32)
+            nc.scalar.activation(out=gate[:], in_=m0[c][:].indirect(list4[:]), func=ACT.Sigmoid,
+                                 bias=bo_t[:, c : c + 1], scale=sp_t[:, c : c + 1])
+            nc.scalar.activation(out=kept[:], in_=m0[c][:].indirect(list3[:]), func=ACT.Copy, scale=so_t[:, c : c + 1])
+            nc.vector.tensor_tensor(out=y[:], in0=kept[:], in1=gate[:], op=ALU.mult)
+            nc.sync.dma_start(out=out[P * c : P * c + P, :], in_=y[:])

@@ -53,10 +53,8 @@ def tile_list_outcomegatedmeet_leaned_kernel(
         xt_s = sb("xt_s", [P, T], U8)
         xo_s = sb("xo_s", [P, T], U8)
         xt_stage = sb("xt_stage", [4, 4, T // 4], I32)
-        w_stage = sb("w_stage", [4, 4, R // 4], I32)
-        pair_stage = sb("pair_stage", [32, 4, R // 4], I32)
-        w_spread = sb("w_spread", [P, R // 4], I32)
-        pair_spread = sb("pair_spread", [P, R // 4], I32)
+        w_stage = sb("w_stage", [32, 4, 2, R // 4], I32)
+        w_spread = sb("w_spread", [P, 2, R // 4], I32)
         w_raw = sb("w_raw", [P, R], U16)
         w2_raw = sb("w2_raw", [P, R], U32)
         w0_raw = sb("w0_raw", [P, R], U32)
@@ -67,40 +65,37 @@ def tile_list_outcomegatedmeet_leaned_kernel(
         pair_s = sb("pair_s", [P, R], U8)
         wb_w = sb("wb_w", [P, N], U16)
         wc_w = sb("wc_w", [P, N], U32)
-        wb_s = sb("wb_s", [P, N], U8)
-        wc_s = sb("wc_s", [P, N], U8)
+        out_s = sb("out_s", [P, N], U8)
         so_t = sb("so_t", [P, 2], F32)
         sp_t = sb("sp_t", [P, 2], F32)
         bo_t = sb("bo_t", [P, 2], F32)
 
-        nc.vector.memset(pair_stage[:], 0)
+        nc.vector.memset(w_stage[:], 0)
         nc.vector.memset(xo_s[:].bitcast(I32), 0)
-        nc.gpsimd.memset(wb_s[:].bitcast(I32), 0)
-        nc.gpsimd.memset(wc_s[:].bitcast(I32), 0)
         nc.vector.memset(xt_s[:].bitcast(I32), 0)
-        nc.vector.memset(w_spread[:], 0)
+        nc.vector.memset(out_s[:].bitcast(I32), 0)
 
         nc.sync.dma_start(list1[:], offs)
         nc.scalar.dma_start(out=xt_stage[:], in_=staged_rows(xt_scales))
-        nc.scalar.dma_start(out=w_stage[:], in_=staged_rows(w_scales))
-        nc.sync.dma_start(out=xt_w[:].bitcast(I32), in_=words32(xt_words))
-        nc.sync.dma_start(out=pair_stage[0:4], in_=staged_rows(w2_scales))
-        nc.sync.dma_start(out=pair_stage[4:8], in_=staged_rows(w0_scales))
+        nc.sync.dma_start(list2[:], offs2)
+        nc.scalar.dma_start(out=w_stage[0:4, :, 0, :], in_=staged_rows(w_scales))
+        nc.scalar.dma_start(out=w_stage[0:4, :, 1, :], in_=staged_rows(w2_scales))
+        nc.scalar.dma_start(out=w_stage[4:8, :, 1, :], in_=staged_rows(w0_scales))
         nc.sync.dma_start(out=w_raw[:].bitcast(I32), in_=w_words[0].bitcast(I32))
+        nc.sync.dma_start(out=xt_w[:].bitcast(I32), in_=words32(xt_words))
         nc.sync.dma_start(out=w2_raw[:].bitcast(I32), in_=words32(w2_words))
+        nc.sync.dma_start(out=w0_raw[:].bitcast(I32), in_=words32(w0_words))
         load_rows(nc.sync, xo_s, 4, xo_scales)
         nc.sync.dma_start(out=xo_w[:].bitcast(I32), in_=words32(xo_words))
-        nc.sync.dma_start(list2[:], offs2)
-        nc.sync.dma_start(out=w0_raw[:].bitcast(I32), in_=words32(w0_words))
         nc.sync.dma_start(out=wb_w[:].bitcast(I32), in_=wb_words[0].bitcast(I32))
         nc.sync.dma_start(out=wc_w[:].bitcast(I32), in_=words32(wc_words))
-        load_rows(nc.gpsimd, wb_s, 0, wb_scales)
-        load_rows(nc.sync, wc_s, 0, wc_scales)
+        load_rows(nc.sync, out_s, 0, wb_scales)
+        load_rows(nc.sync, out_s, 4, wc_scales)
         nc.sync.dma_start(list4[:], offs4)
-        nc.sync.dma_start(list3[:], offs3)
         with nc.allow_non_contiguous_dma(reason="one value a partition"):
-            for queue, tile, vec in ((nc.gpsimd, sp_t, sp), (nc.gpsimd, bo_t, bo), (nc.sync, so_t, so)):
-                queue.dma_start(out=tile[:], in_=vec.rearrange("(c p) o -> p (c o)", p=P))
+            for tile, vec in ((sp_t, sp), (bo_t, bo), (so_t, so)):
+                nc.sync.dma_start(out=tile[:], in_=vec.rearrange("(c p) o -> p (c o)", p=P))
+        nc.sync.dma_start(list3[:], offs3)
 
         def spread(dst, stage, rows):
             for q in range(4):
@@ -110,50 +105,53 @@ def tile_list_outcomegatedmeet_leaned_kernel(
             copy(out=dst.rearrange("p (t m) -> p t m", t=4), in_=src.rearrange("p (m t) -> p t m", t=4))
 
         def deal_by_write(copy, dst, src):
-            copy(out=dst.rearrange("p (t m) -> p m t", t=4), in_=src.rearrange("p (m t) -> p m t", t=4))
+            copy(out=dst.rearrange("p (t g i) -> p g t i", t=4, i=4), in_=src.rearrange("p (g i t) -> p g t i", t=4, i=4))
 
-        def gather(name, words, scales, offsets, h):
-            gw = sb(name + "_gw%d" % h, [P, HALF], U32)
-            gs = sb(name + "_gs%d" % h, [P, HALF], U8)
-            part = offsets[:, 8 * h : 8 * h + 8]
-            nc.vector.tensor_copy(out=gw[:], in_=words[:].indirect(part))
-            nc.vector.tensor_copy(out=gs[:], in_=scales[:].indirect(part))
-            return gw, gs
+        def gather_words(name, words, offsets, h):
+            picked = sb(name + "_gw%d" % h, [P, HALF], U32)
+            nc.vector.tensor_copy(out=picked[:], in_=words[:].indirect(offsets[:, 8 * h : 8 * h + 8]))
+            return picked
+
+        def gather_scales(name, scales, offsets):
+            picked = sb(name + "_gs", [P, J], U8)
+            nc.vector.tensor_copy(out=picked[:], in_=scales[:].indirect(offsets[:]))
+            return picked
 
         spread(xt_s[:].bitcast(I32), xt_stage, 4)
-        spread(w_spread, w_stage, 4)
-        deal_by_read(nc.vector.tensor_copy, w_s[:], w_spread[:].bitcast(U8))
+        spread(w_spread[:].rearrange("p a c -> p (a c)"), w_stage[:].rearrange("p q a c -> p q (a c)"), 32)
+        xt_gs = gather_scales("xt", xt_s, list1)
+        deal_by_read(nc.vector.tensor_copy, w_s[:], w_spread[:, 0, :].bitcast(U8))
         deal_by_read(nc.scalar.copy, w_w[:], w_raw[:])
         deal_by_write(nc.scalar.copy, w2_w[:], w2_raw[:])
+        deal_by_write(nc.scalar.copy, w0_w[:], w0_raw[:])
+        xt_gw = [gather_words("xt", xt_w, list1, 0)]
+        deal_by_read(nc.vector.tensor_copy, pair_s[:], w_spread[:, 1, :].bitcast(U8))
+        xt_gw.append(gather_words("xt", xt_w, list1, 1))
+        xo_gs = gather_scales("xo", xo_s, list2)
+        xo_gw = [gather_words("xo", xo_w, list2, h) for h in range(2)]
 
         a_ps = [psum.tile([P, 4, HALF], F32, name="a_ps%d" % h) for h in range(2)]
         b_ps = [psum.tile([P, 4, HALF], F32, name="b_ps%d" % h) for h in range(2)]
         a_sb = [sb("a_sb%d" % h, [P, HALF, 4], F32) for h in range(2)]
 
-        xg = [gather("xt", xt_w, xt_s, list1, 0)]
-        spread(pair_spread, pair_stage, 32)
-        deal_by_read(nc.vector.tensor_copy, pair_s[:], pair_spread[:].bitcast(U8))
-        xg.append(gather("xt", xt_w, xt_s, list1, 1))
         for h in range(2):
-            gw, gs = xg[h]
             for t in range(4):
                 cols = slice(P * t, P * t + P)
                 nc.tensor.matmul_mx(out=a_ps[h][:, t, :], lhsT=w_w[:, cols].bitcast(E2M1), lhsT_scale=w_s[:, cols],
-                                    rhs=gw[:].bitcast(E5M2), rhs_scale=gs[:], start=True, stop=True)
+                                    rhs=xt_gw[h][:].bitcast(E5M2), rhs_scale=xt_gs[:, HALF * h : HALF * h + HALF],
+                                    start=True, stop=True)
+            nc.scalar.copy(out=a_sb[h][:], in_=a_ps[h][:].rearrange("p t j -> p j t"))
             for t in range(4):
                 cols = slice(P * t, P * t + P)
                 nc.tensor.matmul_mx(out=b_ps[h][:, t, :], lhsT=w2_w[:, cols].bitcast(E4M3), lhsT_scale=pair_s[:, cols],
-                                    rhs=gw[:].bitcast(E5M2), rhs_scale=gs[:], start=(t == 0), stop=False)
-        deal_by_write(nc.scalar.copy, w0_w[:], w0_raw[:])
+                                    rhs=xt_gw[h][:].bitcast(E5M2), rhs_scale=xt_gs[:, HALF * h : HALF * h + HALF],
+                                    start=(t == 0), stop=False)
         for h in range(2):
-            nc.scalar.copy(out=a_sb[h][:], in_=a_ps[h][:].rearrange("p t j -> p j t"))
-        og = [gather("xo", xo_w, xo_s, list2, h) for h in range(2)]
-        for h in range(2):
-            gw, gs = og[h]
             for t in range(4):
                 cols = slice(P * t, P * t + P)
                 nc.tensor.matmul_mx(out=b_ps[h][:, t, :], lhsT=w0_w[:, cols].bitcast(E4M3), lhsT_scale=pair_s[4:P, cols],
-                                    rhs=gw[:].bitcast(E4M3), rhs_scale=gs[4:P, :], start=False, stop=(t == 3))
+                                    rhs=xo_gw[h][:].bitcast(E4M3), rhs_scale=xo_gs[4:P, HALF * h : HALF * h + HALF],
+                                    start=False, stop=(t == 3))
 
         hid = [sb("hid%d" % h, [P, HALF, 4], BF16) for h in range(2)]
         hq_w = [sb("hq_w%d" % h, [P, HALF], U32) for h in range(2)]
@@ -170,9 +168,9 @@ def tile_list_outcomegatedmeet_leaned_kernel(
             for c in range(2):
                 cols = slice(P * c, P * c + P)
                 pq = low_ps[h][:] if c == 0 else high_ps[:, h]
-                nc.tensor.matmul_mx(out=pq[:, 0, :], lhsT=wb_w[:, cols].bitcast(E2M1), lhsT_scale=wb_s[:, cols],
+                nc.tensor.matmul_mx(out=pq[:, 0, :], lhsT=wb_w[:, cols].bitcast(E2M1), lhsT_scale=out_s[:, cols],
                                     rhs=hq_w[h][:].bitcast(E4M3), rhs_scale=hq_s[h][:], start=True, stop=True)
-                nc.tensor.matmul_mx(out=pq[:, 1, :], lhsT=wc_w[:, cols].bitcast(E4M3), lhsT_scale=wc_s[:, cols],
+                nc.tensor.matmul_mx(out=pq[:, 1, :], lhsT=wc_w[:, cols].bitcast(E4M3), lhsT_scale=out_s[4:P, cols],
                                     rhs=hq_w[h][:].bitcast(E4M3), rhs_scale=hq_s[h][:], start=True, stop=True)
         for h in range(2):
             nc.vector.tensor_reduce(out=m0[0][:, HALF * h : HALF * h + HALF], in_=low_ps[h][:].rearrange("p s j -> p j s"),

from contextlib import ExitStack

import concourse.mybir as mybir

F32 = mybir.dt.float32
BF16 = mybir.dt.bfloat16
I32 = mybir.dt.int32
U32 = mybir.dt.uint32
U16 = mybir.dt.uint16
U8 = mybir.dt.uint8
E4M3 = mybir.dt.float8_e4m3fn_x4
E5M2 = mybir.dt.float8_e5m2_x4
E2M1 = mybir.dt.float4_e2m1fn_x4
ACT = mybir.ActivationFunctionType
ALU = mybir.AluOpType

P = 128
T, J, R, N, O = 1024, 256, 512, 256, 128
HALF = 128
FLOPS = 2 * 512 * J * (3 * R + 2 * N)


def tile_list_outcomegatedmeet_leaned_kernel(
    tc, xt_words, xt_scales, xo_words, xo_scales, w_words, w_scales, w2_words, w2_scales,
    w0_words, w0_scales, wb_words, wb_scales, wc_words, wc_scales, so, sp, bo,
    offs, offs2, offs3, offs4, out,
):
    nc = tc.nc
    with ExitStack() as ctx:
        keep = ctx.enter_context(tc.tile_pool(name="keep", bufs=1))
        psum = ctx.enter_context(tc.psum_pool(name="psum", bufs=1))

        def sb(name, shape, dtype):
            return keep.tile(shape, dtype, name=name, align_bytes=64)

        def words32(dram):
            return dram[0].rearrange("p c r -> p (c r)").bitcast(I32)

        def staged_rows(dram):
            return dram[0].bitcast(I32).rearrange("(q r) c -> r q c", r=4)

        def load_rows(queue, plane, first, dram):
            rows = dram[0].bitcast(I32)
            for q in range(4):
                queue.dma_start(out=plane[32 * q + first : 32 * q + first + 4, :].bitcast(I32), in_=rows[4 * q : 4 * q + 4, :])

        list1 = sb("list1", [P, J // 16], U16)
        list2 = sb("list2", [P, J // 16], U16)
        list3 = sb("list3", [P, O // 16], U16)
        list4 = sb("list4", [P, O // 16], U16)
        xt_w = sb("xt_w", [P, T], U32)
        xo_w = sb("xo_w", [P, T], U32)
        xt_s = sb("xt_s", [P, T], U8)
        xo_s = sb("xo_s", [P, T], U8)
        xt_stage = sb("xt_stage", [4, 4, T // 4], I32)
        w_stage = sb("w_stage", [32, 4, 2, R // 4], I32)
        w_spread = sb("w_spread", [P, 2, R // 4], I32)
        w_raw = sb("w_raw", [P, R], U16)
        w2_raw = sb("w2_raw", [P, R], U32)
        w0_raw = sb("w0_raw", [P, R], U32)
        w_w = sb("w_w", [P, R], U16)
        w2_w = sb("w2_w", [P, R], U32)
        w0_w = sb("w0_w", [P, R], U32)
        w_s = sb("w_s", [P, R], U8)
        pair_s = sb("pair_s", [P, R], U8)
        wb_w = sb("wb_w", [P, N], U16)
        wc_w = sb("wc_w", [P, N], U32)
        out_s = sb("out_s", [P, N], U8)
        so_t = sb("so_t", [P, 2], F32)
        sp_t = sb("sp_t", [P, 2], F32)
        bo_t = sb("bo_t", [P, 2], F32)

        nc.vector.memset(w_stage[:], 0)
        nc.vector.memset(xo_s[:].bitcast(I32), 0)
        nc.vector.memset(xt_s[:].bitcast(I32), 0)
        nc.vector.memset(out_s[:].bitcast(I32), 0)

        nc.sync.dma_start(list1[:], offs)
        nc.scalar.dma_start(out=xt_stage[:], in_=staged_rows(xt_scales))
        nc.sync.dma_start(list2[:], offs2)
        nc.scalar.dma_start(out=w_stage[0:4, :, 0, :], in_=staged_rows(w_scales))
        nc.scalar.dma_start(out=w_stage[0:4, :, 1, :], in_=staged_rows(w2_scales))
        nc.scalar.dma_start(out=w_stage[4:8, :, 1, :], in_=staged_rows(w0_scales))
        nc.sync.dma_start(out=w_raw[:].bitcast(I32), in_=w_words[0].bitcast(I32))
        nc.sync.dma_start(out=xt_w[:].bitcast(I32), in_=words32(xt_words))
        nc.sync.dma_start(out=w2_raw[:].bitcast(I32), in_=words32(w2_words))
        nc.sync.dma_start(out=w0_raw[:].bitcast(I32), in_=words32(w0_words))
        load_rows(nc.sync, xo_s, 4, xo_scales)
        nc.sync.dma_start(out=xo_w[:].bitcast(I32), in_=words32(xo_words))
        nc.sync.dma_start(out=wb_w[:].bitcast(I32), in_=wb_words[0].bitcast(I32))
        nc.sync.dma_start(out=wc_w[:].bitcast(I32), in_=words32(wc_words))
        load_rows(nc.sync, out_s, 0, wb_scales)
        load_rows(nc.sync, out_s, 4, wc_scales)
        nc.sync.dma_start(list4[:], offs4)
        with nc.allow_non_contiguous_dma(reason="one value a partition"):
            for tile, vec in ((sp_t, sp), (bo_t, bo), (so_t, so)):
                nc.sync.dma_start(out=tile[:], in_=vec.rearrange("(c p) o -> p (c o)", p=P))
        nc.sync.dma_start(list3[:], offs3)

        def spread(dst, stage, rows):
            for q in range(4):
                nc.vector.tensor_copy(out=dst[32 * q : 32 * q + rows, :], in_=stage[0:rows, q, :])

        def deal_by_read(copy, dst, src):
            copy(out=dst.rearrange("p (t m) -> p t m", t=4), in_=src.rearrange("p (m t) -> p t m", t=4))

        def deal_by_write(copy, dst, src):
            copy(out=dst.rearrange("p (t g i) -> p g t i", t=4, i=4), in_=src.rearrange("p (g i t) -> p g t i", t=4, i=4))

        def gather_words(name, words, offsets, h):
            picked = sb(name + "_gw%d" % h, [P, HALF], U32)
            nc.vector.tensor_copy(out=picked[:], in_=words[:].indirect(offsets[:, 8 * h : 8 * h + 8]))
            return picked

        def gather_scales(name, scales, offsets):
            picked = sb(name + "_gs", [P, J], U8)
            nc.vector.tensor_copy(out=picked[:], in_=scales[:].indirect(offsets[:]))
            return picked

        spread(xt_s[:].bitcast(I32), xt_stage, 4)
        spread(w_spread[:].rearrange("p a c -> p (a c)"), w_stage[:].rearrange("p q a c -> p q (a c)"), 32)
        xt_gs = gather_scales("xt", xt_s, list1)
        deal_by_read(nc.vector.tensor_copy, w_s[:], w_spread[:, 0, :].bitcast(U8))
        deal_by_read(nc.scalar.copy, w_w[:], w_raw[:])
        deal_by_write(nc.scalar.copy, w2_w[:], w2_raw[:])
        deal_by_write(nc.scalar.copy, w0_w[:], w0_raw[:])
        xt_gw = [gather_words("xt", xt_w, list1, 0)]
        deal_by_read(nc.vector.tensor_copy, pair_s[:], w_spread[:, 1, :].bitcast(U8))
        xt_gw.append(gather_words("xt", xt_w, list1, 1))
        xo_gs = gather_scales("xo", xo_s, list2)
        xo_gw = [gather_words("xo", xo_w, list2, h) for h in range(2)]

        a_ps = [psum.tile([P, 4, HALF], F32, name="a_ps%d" % h) for h in range(2)]
        b_ps = [psum.tile([P, 4, HALF], F32, name="b_ps%d" % h) for h in range(2)]
        a_sb = [sb("a_sb%d" % h, [P, HALF, 4], F32) for h in range(2)]

        for h in range(2):
            for t in range(4):
                cols = slice(P * t, P * t + P)
                nc.tensor.matmul_mx(out=a_ps[h][:, t, :], lhsT=w_w[:, cols].bitcast(E2M1), lhsT_scale=w_s[:, cols],
                                    rhs=xt_gw[h][:].bitcast(E5M2), rhs_scale=xt_gs[:, HALF * h : HALF * h + HALF],
                                    start=True, stop=True)
            nc.scalar.copy(out=a_sb[h][:], in_=a_ps[h][:].rearrange("p t j -> p j t"))
            for t in range(4):
                cols = slice(P * t, P * t + P)
                nc.tensor.matmul_mx(out=b_ps[h][:, t, :], lhsT=w2_w[:, cols].bitcast(E4M3), lhsT_scale=pair_s[:, cols],
                                    rhs=xt_gw[h][:].bitcast(E5M2), rhs_scale=xt_gs[:, HALF * h : HALF * h + HALF],
                                    start=(t == 0), stop=False)
        for h in range(2):
            for t in range(4):
                cols = slice(P * t, P * t + P)
                nc.tensor.matmul_mx(out=b_ps[h][:, t, :], lhsT=w0_w[:, cols].bitcast(E4M3), lhsT_scale=pair_s[4:P, cols],
                                    rhs=xo_gw[h][:].bitcast(E4M3), rhs_scale=xo_gs[4:P, HALF * h : HALF * h + HALF],
                                    start=False, stop=(t == 3))

        hid = [sb("hid%d" % h, [P, HALF, 4], BF16) for h in range(2)]
        hq_w = [sb("hq_w%d" % h, [P, HALF], U32) for h in range(2)]
        hq_s = [sb("hq_s%d" % h, [P, HALF], U8) for h in range(2)]
        for h in range(2):
            nc.vector.tensor_tensor(out=hid[h][:], in0=b_ps[h][:].rearrange("p t j -> p j t"), in1=a_sb[h][:], op=ALU.max)
        for h in range(2):
            nc.vector.quantize_mx(out=hq_w[h][:].bitcast(E4M3), scales=hq_s[h][:], in_=hid[h][:].rearrange("p j t -> p (j t)"))

        low_ps = [psum.tile([P, 2, HALF], F32, name="low_ps%d" % h) for h in range(2)]
        high_ps = psum.tile([P, 2, 2, HALF], F32, name="high_ps")
        m0 = [sb("m0_%d" % c, [P, J], F32) for c in range(2)]
        for h in range(2):
            for c in range(2):
                cols = slice(P * c, P * c + P)
                pq = low_ps[h][:] if c == 0 else high_ps[:, h]
                nc.tensor.matmul_mx(out=pq[:, 0, :], lhsT=wb_w[:, cols].bitcast(E2M1), lhsT_scale=out_s[:, cols],
                                    rhs=hq_w[h][:].bitcast(E4M3), rhs_scale=hq_s[h][:], start=True, stop=True)
                nc.tensor.matmul_mx(out=pq[:, 1, :], lhsT=wc_w[:, cols].bitcast(E4M3), lhsT_scale=out_s[4:P, cols],
                                    rhs=hq_w[h][:].bitcast(E4M3), rhs_scale=hq_s[h][:], start=True, stop=True)
        for h in range(2):
            nc.vector.tensor_reduce(out=m0[0][:, HALF * h : HALF * h + HALF], in_=low_ps[h][:].rearrange("p s j -> p j s"),
                                    axis=mybir.AxisListType.X, op=ALU.max)
        nc.vector.tensor_reduce(out=m0[1][:].rearrange("p (h j) -> p h j", h=2), in_=high_ps[:].rearrange("p h s j -> p h j s"),
                                axis=mybir.AxisListType.X, op=ALU.max)

        for c in range(2):
            gate = sb("gate%d" % c, [P, O], F32)
            kept = sb("kept%d" % c, [P, O], F32)
            y = sb("y%d" % c, [P, O], F32)
            nc.scalar.activation(out=gate[:], in_=m0[c][:].indirect(list4[:]), func=ACT.Sigmoid,
                                 bias=bo_t[:, c : c + 1], scale=sp_t[:, c : c + 1])
            nc.scalar.activation(out=kept[:], in_=m0[c][:].indirect(list3[:]), func=ACT.Copy, scale=so_t[:, c : c + 1])
            nc.vector.tensor_tensor(out=y[:], in0=kept[:], in1=gate[:], op=ALU.mult)
            nc.sync.dma_start(out=out[P * c : P * c + P, :], in_=y[:])
